import numpy as np
import ml_dtypes


def mxq(x, axis, fmt="e4m3"):
    dtype, down = {"e4m3": (ml_dtypes.float8_e4m3fn, 7), "e5m2": (ml_dtypes.float8_e5m2, 14)}[fmt]
    v = np.moveaxis(np.asarray(x, np.float32).astype(ml_dtypes.bfloat16).astype(np.float64), axis, -1)
    blocks = v.reshape(v.shape[:-1] + (-1, 32))
    amax = np.abs(blocks).max(-1, keepdims=True)
    byte = np.maximum(np.where(amax > 0, np.frexp(amax)[1] - 1 + 127, 0) - down, 1)
    scale = np.exp2(byte - 127.0)
    codes = (blocks / scale).astype(np.float32).astype(dtype).astype(np.float64)
    return np.moveaxis((codes * scale).reshape(v.shape), -1, axis)


WIDE = False


def mx_kscale(k):
    if not WIDE:
        return np.ones(k)
    levels = np.array([24, -24, 12, -12, 0])
    if k % 512:
        return np.exp2(np.random.permutation(np.resize(levels, k // 32))).repeat(32)
    a = np.empty((k // 512, 16))
    for p in range(k // 512):
        a[p, :8] = np.random.permutation(np.resize(levels, 8))
        for g in range(8):
            far = levels[np.abs(levels - a[p, g]) >= 10]
            a[p, g + 8] = far[np.random.randint(len(far))]
    return np.exp2(a.ravel()).repeat(32)


def f64(x):
    return np.asarray(x).astype(np.float64)


def striped(idx):
    return np.tile(idx.reshape(-1, 16).T, (8, 1)).astype(np.uint16)


def unstriped(offs):
    return offs[:16].T.reshape(-1).astype(np.int64)


E2M1 = np.array([0.0, 0.5, 1.0, 1.5, 2.0, 3.0, 4.0, 6.0, -0.0, -0.5, -1.0, -1.5, -2.0, -3.0, -4.0, -6.0])


def pack_weight(w, fmt):
    k, n = w.shape
    w = f64(np.asarray(w, np.float32).astype(ml_dtypes.bfloat16)).reshape(k // 32, 32, n)
    amax = np.abs(w).max(1)
    if fmt == "e4m3":
        byte = np.frexp(amax)[1] - 1 + 127 - 7
    else:
        mant, ex = np.frexp(amax / 6.0)
        byte = np.where(mant > 0.5, ex, ex - 1) + 127
    byte = np.clip(np.where(amax > 0, byte, 1), 1, 254)
    scaled = (w * np.exp2(127.0 - byte)[:, None, :]).reshape(k, n).astype(np.float32)
    by_word = np.ascontiguousarray(scaled.reshape(k // 512, 128, 4, n).transpose(0, 1, 3, 2))
    if fmt == "e4m3":
        words = by_word.astype(ml_dtypes.float8_e4m3fn).view(np.uint8)
    else:
        c = by_word.astype(ml_dtypes.float4_e2m1fn).view(np.uint8) & 0xF
        words = (c[..., 0::2] | (c[..., 1::2] << 4)).reshape(k // 512, 128, 2 * n)
    return np.ascontiguousarray(words), np.ascontiguousarray(byte.astype(np.uint8).reshape(k // 512, 16, n))


def unpack_weight(words, scales, fmt):
    g, _, n = scales.shape
    words = np.ascontiguousarray(words).reshape(g, 128, n, -1)
    if fmt == "e4m3":
        vals = words.view(ml_dtypes.float8_e4m3fn).astype(np.float64)
    else:
        nib = np.empty((g, 128, n, 4), np.uint8)
        nib[..., 0::2] = words & 0xF
        nib[..., 1::2] = words >> 4
        vals = E2M1[nib]
    vals = vals * np.repeat(np.exp2(scales.astype(np.float64) - 127.0), 8, axis=1)[..., None]
    return vals.transpose(0, 1, 3, 2).reshape(g * 512, n)


def pack_table4(v):
    words, scales = pack_weight(v, "e2m1")
    g, t = words.shape[0] // 2, v.shape[1]
    return np.ascontiguousarray(words.reshape(g, 2, 128, t, 2).transpose(0, 2, 3, 1, 4).reshape(g, 128, t, 4)), scales


def unpack_table4(words, scales):
    g, _, t, _ = words.shape
    return unpack_weight(words.reshape(g, 128, t, 2, 2).transpose(0, 3, 1, 2, 4).reshape(2 * g, 128, 2 * t), scales, "e2m1")


K, N, T, J = 1024, 512, 4096, 1024


def setup_inputs():
    n = np.random.standard_normal
    s = mx_kscale(K)[:, None]
    p_tab = pack_table4(n((K, T)) * s)
    p_tab2 = pack_table4(n((K, T)) * s)
    p_wi = pack_weight(n((K, N)) / np.sqrt(2 * K) / s, "e4m3")
    return {
        "tab_words": p_tab[0],
        "tab_scales": p_tab[1],
        "tab2_words": p_tab2[0],
        "tab2_scales": p_tab2[1],
        "wr": (n((K, N)) / np.sqrt(2 * K) / s).astype(np.float32),
        "wi_words": p_wi[0],
        "wi_scales": p_wi[1],
        "offs": striped(np.random.permutation(T)[:J]),
    }


def reference(tab_words, tab_scales, tab2_words, tab2_scales, wr, wi_words, wi_scales, offs):
    idx = unstriped(offs)
    tab_ = unpack_table4(tab_words, tab_scales)[:, idx]
    tab2_ = unpack_table4(tab2_words, tab2_scales)[:, idx]
    wr_ = mxq(f64(wr), 0, "e4m3")
    wi_ = unpack_weight(wi_words, wi_scales, "e4m3")
    rr = wr_.T @ tab_
    ii = wi_.T @ tab2_
    zr = rr - ii
    ri = wr_.T @ tab2_ + wi_.T @ tab_
    zi = ri
    return (zr) ** 2 + (zi) ** 2

@@ -1,0 +1,220 @@
+from contextlib import ExitStack
+
+import concourse.mybir as mybir
+
+K, N, T, J = 1024, 512, 4096, 1024
+FLOPS = 4 * 2 * K * N * J
+
+F32 = mybir.dt.float32
+BF16 = mybir.dt.bfloat16
+I32 = mybir.dt.int32
+U32 = mybir.dt.uint32
+U16 = mybir.dt.uint16
+U8 = mybir.dt.uint8
+FP8X4 = mybir.dt.float8_e4m3fn_x4
+FP4X4 = mybir.dt.float4_e2m1fn_x4
+ALU = mybir.AluOpType
+ACT = mybir.ActivationFunctionType
+
+P = 128
+PACK = 4
+PASSES = 2
+M = 128
+CHUNKS = N // M
+HALF = 512
+HALVES = J // HALF
+LIVE = 100
+
+
+def tile_list_cpxtab_pow_kernel(
+    tc, tab_words, tab_scales, tab2_words, tab2_scales, wr, wi_words, wi_scales, offs, out
+):
+    nc = tc.nc
+    with ExitStack() as ctx:
+        keep = ctx.enter_context(tc.tile_pool(name="keep", bufs=1))
+        ring = ctx.enter_context(tc.tile_pool(name="ring", bufs=2))
+        psum = ctx.enter_context(tc.psum_pool(name="psum", bufs=1))
+
+        offsets = keep.tile([P, J // 16], U16, name="offsets")
+        nc.sync.dma_start(offsets[:], offs)
+
+        def zeroed(shape, name, tag):
+            t = keep.tile(shape, U8, name=name, tag=tag, align_bytes=64)
+            nc.vector.memset(t[:].bitcast(I32), 0)
+            return t
+
+        def load_words(words, name, tag):
+            t = keep.tile([P, T], I32, name=name, tag=tag, align_bytes=64)
+            nc.sync.dma_start(t[:], words[0].rearrange("p t b -> p (t b)").bitcast(I32))
+            return t
+
+        def load_scale_rows(queue, window, scales, first):
+            rows = scales.rearrange("a (q r) t -> r q a t", r=4)
+            for r in range(4):
+                queue.dma_start(window[first + r : P : 16, :].bitcast(I32), rows[r].bitcast(I32))
+
+        def gather_scales(window, name):
+            g = keep.tile([P, J], U8, name=name, align_bytes=64)
+            nc.vector.tensor_copy(g[:], window[:].indirect(offsets[:]))
+            return g
+
+        def move_plane(plane, g, shift):
+            nc.scalar.dma_start(plane[0:LIVE, :].bitcast(I32), g[shift : shift + LIVE, :].bitcast(I32))
+
+        def gather_words(window, h, name):
+            g = ring.tile([P, HALF], I32, name="pairs", align_bytes=64)
+            cols = slice(h * HALF // 16, (h + 1) * HALF // 16)
+            nc.vector.tensor_copy(g[:].bitcast(U32), window[:].bitcast(U32).indirect(offsets[:, cols]))
+            parted = keep.tile([P, PASSES, HALF], U16, name=name, align_bytes=64)
+            nc.vector.tensor_copy(parted[:], g[:].bitcast(U16).rearrange("p (j d) -> p d j", d=PASSES))
+            return parted
+
+        wr_rows = wr.rearrange("(a p t) n -> a p t n", a=PASSES, t=PACK)
+
+        def load_wr(a, c0, c1, name, tag):
+            raw = keep.tile([P, PACK, (c1 - c0) * M], F32, name=name, tag=tag, align_bytes=64)
+            nc.sync.dma_start(raw[:], wr_rows[a, :, :, c0 * M : c1 * M])
+            return raw
+
+        def quantise(raw, c, name):
+            pos = ring.tile([P, PASSES, M, PACK], BF16, name="pos", align_bytes=64)
+            neg = ring.tile([P, PASSES, M, PACK], BF16, name="neg", align_bytes=64)
+            for a in range(PASSES):
+                nc.scalar.copy(
+                    pos[:, a].rearrange("p (c i) t -> p c t i", i=4),
+                    raw[a][:, :, c * M : (c + 1) * M].rearrange("p t (c i) -> p c t i", i=4),
+                )
+            flat_pos = pos[:].rearrange("p a n t -> p (a n t)")
+            flat_neg = neg[:].rearrange("p a n t -> p (a n t)")
+            nc.vector.tensor_scalar(flat_neg, flat_pos, -1.0, None, ALU.mult)
+            both = []
+            for flat, sign in ((flat_pos, "pos"), (flat_neg, "neg")):
+                codes = keep.tile([P, PASSES * M], U32, name=name + sign + "_codes", align_bytes=64)
+                scales = keep.tile([P, PASSES * M], U8, name=name + sign + "_scales", align_bytes=64)
+                nc.vector.quantize_mx(out=codes[:].bitcast(FP8X4), scales=scales[:], in_=flat)
+                both.append(
+                    [(codes[:, a * M : (a + 1) * M], scales[:, a * M : (a + 1) * M]) for a in range(PASSES)]
+                )
+            return both
+
+        def product(bank, weight, words, planes, h, start, stop, j0=0, j1=HALF):
+            for a in range(PASSES):
+                nc.tensor.matmul_mx(
+                    out=bank[:, 0 : j1 - j0],
+                    lhsT=weight[a][0].bitcast(FP8X4),
+                    lhsT_scale=weight[a][1],
+                    rhs=words[:, a, j0:j1].bitcast(FP4X4),
+                    rhs_scale=planes[a][:, h * HALF + j0 : h * HALF + j1],
+                    start=start and a == 0,
+                    stop=stop and a == PASSES - 1,
+                )
+
+        re_scale_win = zeroed([P, T], "re_scale_win", "shared_a")
+        wi_planes = zeroed([P, PASSES * N], "wi_planes", "wi_planes")
+        re_plane1 = zeroed([P, J], "re_plane1", "re_plane1")
+        im_plane0 = zeroed([P, J], "im_plane0", "im_plane0")
+        im_plane1 = zeroed([P, J], "im_plane1", "im_plane1")
+        im_scale_win = zeroed([P, T], "im_scale_win", "im_scale_win")
+
+        wi_codes = keep.tile([P, PASSES, N], I32, name="wi_codes", align_bytes=64)
+        nc.sync.dma_start(wi_codes[:], wi_words.rearrange("a p n i -> p a (n i)").bitcast(I32))
+        raw0 = [load_wr(0, 0, 1, "raw0a", "raw_a")]
+        load_scale_rows(nc.sync, re_scale_win, tab_scales, 0)
+        re_win = load_words(tab_words, "re_win", "shared_b")
+        raw0.append(load_wr(1, 0, 1, "raw0b", "raw_b"))
+        load_scale_rows(nc.scalar, im_scale_win, tab2_scales, 8)
+        wi_rows = wi_scales.rearrange("a (q r) n -> r q a n", r=4)
+        for r in range(4):
+            nc.gpsimd.dma_start(
+                wi_planes[r:P:32, :].bitcast(I32).rearrange("q (a n) -> q a n", a=PASSES), wi_rows[r].bitcast(I32)
+            )
+        wi = [
+            [
+                (wi_codes[:, a, c * M : (c + 1) * M], wi_planes[:, a * N + c * M : a * N + (c + 1) * M])
+                for a in range(PASSES)
+            ]
+            for c in range(CHUNKS)
+        ]
+
+        re_plane0 = gather_scales(re_scale_win, "re_plane0")
+        im_win = load_words(tab2_words, "im_win", "shared_a")
+        move_plane(re_plane1, re_plane0, 16)
+        re_planes = [re_plane0, re_plane1]
+        im_rows = gather_scales(im_scale_win, "im_rows")
+        move_plane(im_plane0, im_rows, 8)
+        move_plane(im_plane1, im_rows, 24)
+        im_planes = [im_plane0, im_plane1]
+        re = [gather_words(re_win, h, "re%d" % h) for h in range(HALVES)]
+        wq = [quantise(raw0, 0, "wr0")]
+        raw1 = [load_wr(0, 1, 2, "raw1a", "im_scale_win"), load_wr(1, 1, 2, "raw1b", "raw_b")]
+        both23 = keep.tile([P, PASSES, PACK, 2 * M], F32, name="raw23", tag="shared_b", align_bytes=64)
+        for a in range(PASSES):
+            nc.sync.dma_start(both23[:, a], wr_rows[a, :, :, 2 * M : 4 * M])
+        raw23 = [both23[:, a] for a in range(PASSES)]
+
+        tiles = [(c, h) for c in range(CHUNKS) for h in range(HALVES)]
+        free = list(range(8))
+        zi = {}
+        zr = {}
+
+        def take(kind, t):
+            b = free.pop(0)
+            return b, psum.tile([M, HALF], F32, name="%s%d%d" % (kind, t[0], t[1]), tag="bank%d" % b)
+
+        early = sorted(tiles[:-1], key=lambda t: t[1])
+        for t in early:
+            zi[t] = take("zi", t)
+            product(zi[t][1], wi[t[0]], re[t[1]], re_planes, t[1], True, False)
+        zr[tiles[0]] = take("zr", tiles[0])
+        product(zr[tiles[0]][1], wq[0][1], re[0], re_planes, 0, True, False)
+
+        im = [gather_words(im_win, h, "im%d" % h) for h in range(HALVES)]
+        wq.append(quantise(raw1, 0, "wr1"))
+
+        def square(slot, name):
+            sq = ring.tile([M, HALF], F32, name=name)
+            nc.scalar.activation(sq[:], slot[1][:], ACT.Square)
+            free.append(slot[0])
+            return sq
+
+        for i, t in enumerate(tiles[:-1]):
+            c, h = t
+            if i in (2, 4):
+                wq.append(quantise(raw23, i // 2 - 1, "wr%d" % (i // 2 + 1)))
+            if i == 0:
+                product(zi[t][1], wq[c][0], im[h], im_planes, h, False, True)
+                zi_sq = square(zi[t], "zi_sq")
+                product(zr[t][1], wi[c], im[h], im_planes, h, False, True)
+            elif i == 1:
+                zr[t] = take("zr", t)
+                product(zr[t][1], wq[c][1], re[h], re_planes, h, True, False)
+                product(zi[t][1], wq[c][0], im[h], im_planes, h, False, True)
+                zi_sq = square(zi[t], "zi_sq")
+                product(zr[t][1], wi[c], im[h], im_planes, h, False, True)
+            else:
+                zr[t] = take("zr", t)
+                product(zr[t][1], wi[c], im[h], im_planes, h, True, False)
+                if i == 2:
+                    last = tiles[-1]
+                    zi[last] = take("zi", last)
+                    product(zi[last][1], wi[last[0]], re[last[1]], re_planes, last[1], True, False)
+                product(zi[t][1], wq[c][0], im[h], im_planes, h, False, True)
+                zi_sq = square(zi[t], "zi_sq")
+                product(zr[t][1], wq[c][1], re[h], re_planes, h, False, True)
+            zr_sq = square(zr[t], "zr_sq")
+            power = ring.tile([M, HALF], F32, name="power", bufs=4)
+            nc.vector.tensor_tensor(power[:], zr_sq[:], zi_sq[:], ALU.add)
+            nc.sync.dma_start(out[c * M : (c + 1) * M, h * HALF : (h + 1) * HALF], power[:])
+
+        c, h = tiles[-1]
+        product(zi[tiles[-1]][1], wq[c][0], im[h], im_planes, h, False, True)
+        zi_sq = square(zi[tiles[-1]], "zi_sq")
+        for j0 in range(0, HALF, M):
+            b, bank = take("zr_end", (c, j0 // M))
+            product(bank, wi[c], im[h], im_planes, h, True, False, j0, j0 + M)
+            product(bank, wq[c][1], re[h], re_planes, h, False, True, j0, j0 + M)
+            zr_end = ring.tile([M, M], F32, name="zr_end", bufs=4)
+            nc.scalar.activation(zr_end[:], bank[:, 0:M], ACT.Square)
+            power_end = ring.tile([M, M], F32, name="power_end", bufs=4)
+            nc.vector.tensor_tensor(power_end[:], zr_end[:], zi_sq[:, j0 : j0 + M], ALU.add)
+            nc.sync.dma_start(out[c * M : (c + 1) * M, h * HALF + j0 : h * HALF + j0 + M], power_end[:])

@@ -59,14 +59,18 @@ def tile_list_cpxtab_pow_kernel(
             return g
 
         def move_plane(plane, g, shift):
-            nc.scalar.dma_start(plane[0:LIVE, :].bitcast(I32), g[shift : shift + LIVE, :].bitcast(I32))
+            nc.sync.dma_start(plane[0:LIVE, :].bitcast(I32), g[shift : shift + LIVE, :].bitcast(I32))
 
         def gather_words(window, h, name):
-            g = ring.tile([P, HALF], I32, name="pairs", align_bytes=64)
+            g = keep.tile([P, HALF], I32, name="pairs", align_bytes=64)
             cols = slice(h * HALF // 16, (h + 1) * HALF // 16)
             nc.vector.tensor_copy(g[:].bitcast(U32), window[:].bitcast(U32).indirect(offsets[:, cols]))
-            parted = keep.tile([P, PASSES, HALF], U16, name=name, align_bytes=64)
-            nc.vector.tensor_copy(parted[:], g[:].bitcast(U16).rearrange("p (j d) -> p d j", d=PASSES))
+            by_pass = g[:].bitcast(U16).rearrange("p (j d) -> p d j", d=PASSES)
+            parted = []
+            for a in range(PASSES):
+                words = keep.tile([P, HALF], U16, name="%s_%d" % (name, a), align_bytes=64)
+                nc.vector.tensor_copy(words[:], by_pass[:, a, :])
+                parted.append(words)
             return parted
 
         wr_rows = wr.rearrange("(a p t) n -> a p t n", a=PASSES, t=PACK)
@@ -103,31 +107,30 @@ def tile_list_cpxtab_pow_kernel(
                     out=bank[:, 0 : j1 - j0],
                     lhsT=weight[a][0].bitcast(FP8X4),
                     lhsT_scale=weight[a][1],
-                    rhs=words[:, a, j0:j1].bitcast(FP4X4),
+                    rhs=words[a][:, j0:j1].bitcast(FP4X4),
                     rhs_scale=planes[a][:, h * HALF + j0 : h * HALF + j1],
                     start=start and a == 0,
                     stop=stop and a == PASSES - 1,
                 )
 
         re_scale_win = zeroed([P, T], "re_scale_win", "shared_a")
+        im_scale_win = zeroed([P, T], "im_scale_win", "im_scale_win")
         wi_planes = zeroed([P, PASSES * N], "wi_planes", "wi_planes")
         re_plane1 = zeroed([P, J], "re_plane1", "re_plane1")
-        im_plane0 = zeroed([P, J], "im_plane0", "im_plane0")
         im_plane1 = zeroed([P, J], "im_plane1", "im_plane1")
-        im_scale_win = zeroed([P, T], "im_scale_win", "im_scale_win")
 
         wi_codes = keep.tile([P, PASSES, N], I32, name="wi_codes", align_bytes=64)
         nc.sync.dma_start(wi_codes[:], wi_words.rearrange("a p n i -> p a (n i)").bitcast(I32))
-        raw0 = [load_wr(0, 0, 1, "raw0a", "raw_a")]
+        raw0 = [load_wr(0, 0, 1, "raw0_0", "raw0_0")]
         load_scale_rows(nc.sync, re_scale_win, tab_scales, 0)
+        load_scale_rows(nc.sync, im_scale_win, tab2_scales, 0)
         re_win = load_words(tab_words, "re_win", "shared_b")
-        raw0.append(load_wr(1, 0, 1, "raw0b", "raw_b"))
-        load_scale_rows(nc.scalar, im_scale_win, tab2_scales, 8)
         wi_rows = wi_scales.rearrange("a (q r) n -> r q a n", r=4)
         for r in range(4):
-            nc.gpsimd.dma_start(
+            nc.sync.dma_start(
                 wi_planes[r:P:32, :].bitcast(I32).rearrange("q (a n) -> q a n", a=PASSES), wi_rows[r].bitcast(I32)
             )
+        raw0.append(load_wr(1, 0, 1, "raw0_1", "raw0_1"))
         wi = [
             [
                 (wi_codes[:, a, c * M : (c + 1) * M], wi_planes[:, a * N + c * M : a * N + (c + 1) * M])
@@ -137,16 +140,18 @@ def tile_list_cpxtab_pow_kernel(
         ]
 
         re_plane0 = gather_scales(re_scale_win, "re_plane0")
-        im_win = load_words(tab2_words, "im_win", "shared_a")
         move_plane(re_plane1, re_plane0, 16)
+        im_win = load_words(tab2_words, "im_win", "shared_a")
         re_planes = [re_plane0, re_plane1]
-        im_rows = gather_scales(im_scale_win, "im_rows")
-        move_plane(im_plane0, im_rows, 8)
-        move_plane(im_plane1, im_rows, 24)
+        im_plane0 = gather_scales(im_scale_win, "im_plane0")
+        move_plane(im_plane1, im_plane0, 16)
         im_planes = [im_plane0, im_plane1]
         re = [gather_words(re_win, h, "re%d" % h) for h in range(HALVES)]
         wq = [quantise(raw0, 0, "wr0")]
-        raw1 = [load_wr(0, 1, 2, "raw1a", "im_scale_win"), load_wr(1, 1, 2, "raw1b", "raw_b")]
+        both1 = keep.tile([P, PASSES, PACK, M], F32, name="raw1", tag="im_scale_win", align_bytes=64)
+        for a in range(PASSES):
+            nc.sync.dma_start(both1[:, a], wr_rows[a, :, :, M : 2 * M])
+        raw1 = [both1[:, a] for a in range(PASSES)]
         both23 = keep.tile([P, PASSES, PACK, 2 * M], F32, name="raw23", tag="shared_b", align_bytes=64)
         for a in range(PASSES):
             nc.sync.dma_start(both23[:, a], wr_rows[a, :, :, 2 * M : 4 * M])

@@ -18,12 +18,18 @@ ACT = mybir.ActivationFunctionType
 
 P = 128
 PACK = 4
-PASSES = 2
+PASSES = K // (P * PACK)
+LIVE_ROWS = 4
+SECOND_PASS_ROW = 16
+LIST_ROWS = 16
 M = 128
-CHUNKS = N // M
 HALF = 512
 HALVES = J // HALF
-LIVE = 100
+BANKS = 8
+SIDE_CHUNKS = BANKS // (2 * HALVES)
+WIDE = SIDE_CHUNKS * M
+LINE = 4
+STAGES = 4
 
 
 def tile_list_cpxtab_pow_kernel(
@@ -35,37 +41,37 @@ def tile_list_cpxtab_pow_kernel(
         ring = ctx.enter_context(tc.tile_pool(name="ring", bufs=2))
         psum = ctx.enter_context(tc.psum_pool(name="psum", bufs=1))
 
-        offsets = keep.tile([P, J // 16], U16, name="offsets")
+        offsets = keep.tile([P, J // LIST_ROWS], U16, name="offsets")
         nc.sync.dma_start(offsets[:], offs)
 
-        def zeroed(shape, name, tag):
-            t = keep.tile(shape, U8, name=name, tag=tag, align_bytes=64)
-            nc.vector.memset(t[:].bitcast(I32), 0)
-            return t
+        def zeroed(columns, name, tag):
+            cleared = keep.tile([P, columns], U8, name=name, tag=tag, align_bytes=64)
+            nc.vector.memset(cleared[:].bitcast(I32), 0)
+            return cleared
 
-        def load_words(words, name, tag):
-            t = keep.tile([P, T], I32, name=name, tag=tag, align_bytes=64)
-            nc.sync.dma_start(t[:], words[0].rearrange("p t b -> p (t b)").bitcast(I32))
-            return t
+        def load_table_words(words, name, tag):
+            window = keep.tile([P, T], I32, name=name, tag=tag, align_bytes=64)
+            nc.sync.dma_start(window[:], words[0].rearrange("p t b -> p (t b)").bitcast(I32))
+            return window
 
-        def load_scale_rows(queue, window, scales, first):
-            rows = scales.rearrange("a (q r) t -> r q a t", r=4)
-            for r in range(4):
-                queue.dma_start(window[first + r : P : 16, :].bitcast(I32), rows[r].bitcast(I32))
+        def load_table_scales(window, scales):
+            rows = scales.rearrange("a (q r) t -> r q a t", r=LIVE_ROWS)
+            for r in range(LIVE_ROWS):
+                nc.sync.dma_start(window[r:P:SECOND_PASS_ROW, :].bitcast(I32), rows[r].bitcast(I32))
 
-        def gather_scales(window, name):
-            g = keep.tile([P, J], U8, name=name, align_bytes=64)
-            nc.vector.tensor_copy(g[:], window[:].indirect(offsets[:]))
-            return g
-
-        def move_plane(plane, g, shift):
-            nc.sync.dma_start(plane[0:LIVE, :].bitcast(I32), g[shift : shift + LIVE, :].bitcast(I32))
+        def gather_planes(window, second, name):
+            first = keep.tile([P, J], U8, name=name, align_bytes=64)
+            nc.vector.tensor_copy(first[:], window[:].indirect(offsets[:]))
+            nc.sync.dma_start(
+                second[0 : P - SECOND_PASS_ROW, :].bitcast(I32), first[SECOND_PASS_ROW:P, :].bitcast(I32)
+            )
+            return [first, second]
 
         def gather_words(window, h, name):
-            g = keep.tile([P, HALF], I32, name="pairs", align_bytes=64)
-            cols = slice(h * HALF // 16, (h + 1) * HALF // 16)
-            nc.vector.tensor_copy(g[:].bitcast(U32), window[:].bitcast(U32).indirect(offsets[:, cols]))
-            by_pass = g[:].bitcast(U16).rearrange("p (j d) -> p d j", d=PASSES)
+            pairs = keep.tile([P, HALF], I32, name="pairs", align_bytes=64)
+            entries = slice(h * HALF // LIST_ROWS, (h + 1) * HALF // LIST_ROWS)
+            nc.vector.tensor_copy(pairs[:].bitcast(U32), window[:].bitcast(U32).indirect(offsets[:, entries]))
+            by_pass = pairs[:].bitcast(U16).rearrange("p (j a) -> p a j", a=PASSES)
             parted = []
             for a in range(PASSES):
                 words = keep.tile([P, HALF], U16, name="%s_%d" % (name, a), align_bytes=64)
@@ -74,32 +80,41 @@ def tile_list_cpxtab_pow_kernel(
             return parted
 
         wr_rows = wr.rearrange("(a p t) n -> a p t n", a=PASSES, t=PACK)
+        wi_by_partition = wi_words.rearrange("a p n t -> p a (n t)").bitcast(I32)
 
-        def load_wr(a, c0, c1, name, tag):
-            raw = keep.tile([P, PACK, (c1 - c0) * M], F32, name=name, tag=tag, align_bytes=64)
-            nc.sync.dma_start(raw[:], wr_rows[a, :, :, c0 * M : c1 * M])
-            return raw
-
-        def quantise(raw, c, name):
-            pos = ring.tile([P, PASSES, M, PACK], BF16, name="pos", align_bytes=64)
-            neg = ring.tile([P, PASSES, M, PACK], BF16, name="neg", align_bytes=64)
-            for a in range(PASSES):
-                nc.scalar.copy(
-                    pos[:, a].rearrange("p (c i) t -> p c t i", i=4),
-                    raw[a][:, :, c * M : (c + 1) * M].rearrange("p t (c i) -> p c t i", i=4),
+        def load_wi_side(side, tag):
+            codes = keep.tile([P, PASSES, WIDE], I32, name="wi_codes%d" % side, tag=tag, align_bytes=64)
+            nc.sync.dma_start(codes[:], wi_by_partition[:, :, side * WIDE : (side + 1) * WIDE])
+            chunks = []
+            for u in range(SIDE_CHUNKS):
+                n0 = side * WIDE + u * M
+                chunks.append(
+                    [(codes[:, a, u * M : (u + 1) * M], wi_planes[:, a * N + n0 : a * N + n0 + M]) for a in range(PASSES)]
                 )
-            flat_pos = pos[:].rearrange("p a n t -> p (a n t)")
-            flat_neg = neg[:].rearrange("p a n t -> p (a n t)")
+            return chunks
+
+        def quantise(raw, name):
+            pos = ring.tile([P, WIDE, PACK], BF16, name="pos", align_bytes=64)
+            neg = ring.tile([P, WIDE, PACK], BF16, name="neg", align_bytes=64)
+            nc.scalar.copy(
+                pos[:].rearrange("p (c i) t -> p c t i", i=LINE), raw.rearrange("p t (c i) -> p c t i", i=LINE)
+            )
+            flat_pos = pos[:].rearrange("p n t -> p (n t)")
+            flat_neg = neg[:].rearrange("p n t -> p (n t)")
             nc.vector.tensor_scalar(flat_neg, flat_pos, -1.0, None, ALU.mult)
-            both = []
+            signs = []
             for flat, sign in ((flat_pos, "pos"), (flat_neg, "neg")):
-                codes = keep.tile([P, PASSES * M], U32, name=name + sign + "_codes", align_bytes=64)
-                scales = keep.tile([P, PASSES * M], U8, name=name + sign + "_scales", align_bytes=64)
-                nc.vector.quantize_mx(out=codes[:].bitcast(FP8X4), scales=scales[:], in_=flat)
-                both.append(
-                    [(codes[:, a * M : (a + 1) * M], scales[:, a * M : (a + 1) * M]) for a in range(PASSES)]
-                )
-            return both
+                codes = keep.tile([P, WIDE], U32, name=name + sign + "_codes", align_bytes=64)
+                plane = keep.tile([P, WIDE], U8, name=name + sign + "_plane", align_bytes=64)
+                nc.vector.quantize_mx(out=codes[:].bitcast(FP8X4), scales=plane[:], in_=flat)
+                signs.append((codes, plane))
+            return signs
+
+        def chunks_of(quantised, sign):
+            return [
+                [[part[:, u * M : (u + 1) * M] for part in quantised[a][sign]] for a in range(PASSES)]
+                for u in range(SIDE_CHUNKS)
+            ]
 
         def product(bank, weight, words, planes, h, start, stop, j0=0, j1=HALF):
             for a in range(PASSES):
@@ -113,113 +128,100 @@ def tile_list_cpxtab_pow_kernel(
                     stop=stop and a == PASSES - 1,
                 )
 
-        re_scale_win = zeroed([P, T], "re_scale_win", "shared_a")
-        im_scale_win = zeroed([P, T], "im_scale_win", "im_scale_win")
-        wi_planes = zeroed([P, PASSES * N], "wi_planes", "wi_planes")
-        re_plane1 = zeroed([P, J], "re_plane1", "re_plane1")
-        im_plane1 = zeroed([P, J], "im_plane1", "im_plane1")
+        re_scale_window = zeroed(T, "re_scale_window", "then_im_words")
+        im_scale_window = zeroed(T, "im_scale_window", "then_wi_side1")
+        wi_planes = zeroed(PASSES * N, "wi_planes", "wi_planes")
+        re_second_plane = zeroed(J, "re_second_plane", "re_second_plane")
+        im_second_plane = zeroed(J, "im_second_plane", "im_second_plane")
 
-        wi_codes = keep.tile([P, PASSES, N], I32, name="wi_codes", align_bytes=64)
-        nc.sync.dma_start(wi_codes[:], wi_words.rearrange("a p n i -> p a (n i)").bitcast(I32))
-        raw0 = [load_wr(0, 0, 1, "raw0_0", "raw0_0")]
-        load_scale_rows(nc.sync, re_scale_win, tab_scales, 0)
-        load_scale_rows(nc.sync, im_scale_win, tab2_scales, 0)
-        re_win = load_words(tab_words, "re_win", "shared_b")
-        wi_rows = wi_scales.rearrange("a (q r) n -> r q a n", r=4)
-        for r in range(4):
+        wi = load_wi_side(0, "wi_side0")
+        raw_side0 = [keep.tile([P, PACK, WIDE], F32, name="raw_side0_%d" % a, align_bytes=64) for a in range(PASSES)]
+        nc.sync.dma_start(raw_side0[0][:], wr_rows[0, :, :, 0:WIDE])
+        load_table_scales(re_scale_window, tab_scales)
+        load_table_scales(im_scale_window, tab2_scales)
+        wi_scale_rows = wi_scales.rearrange("a (q r) n -> r q a n", r=LIVE_ROWS)
+        for r in range(LIVE_ROWS):
             nc.sync.dma_start(
-                wi_planes[r:P:32, :].bitcast(I32).rearrange("q (a n) -> q a n", a=PASSES), wi_rows[r].bitcast(I32)
+                wi_planes[r:P:32, :].bitcast(I32).rearrange("q (a n) -> q a n", a=PASSES),
+                wi_scale_rows[r].bitcast(I32),
             )
-        raw0.append(load_wr(1, 0, 1, "raw0_1", "raw0_1"))
-        wi = [
-            [
-                (wi_codes[:, a, c * M : (c + 1) * M], wi_planes[:, a * N + c * M : a * N + (c + 1) * M])
-                for a in range(PASSES)
-            ]
-            for c in range(CHUNKS)
-        ]
+        re_window = load_table_words(tab_words, "re_window", "then_raw_side1")
+        nc.sync.dma_start(raw_side0[1][:], wr_rows[1, :, :, 0:WIDE])
 
-        re_plane0 = gather_scales(re_scale_win, "re_plane0")
-        move_plane(re_plane1, re_plane0, 16)
-        im_win = load_words(tab2_words, "im_win", "shared_a")
-        re_planes = [re_plane0, re_plane1]
-        im_plane0 = gather_scales(im_scale_win, "im_plane0")
-        move_plane(im_plane1, im_plane0, 16)
-        im_planes = [im_plane0, im_plane1]
-        re = [gather_words(re_win, h, "re%d" % h) for h in range(HALVES)]
-        wq = [quantise(raw0, 0, "wr0")]
-        both1 = keep.tile([P, PASSES, PACK, M], F32, name="raw1", tag="im_scale_win", align_bytes=64)
+        re_planes = gather_planes(re_scale_window, re_second_plane, "re_first_plane")
+        im_window = load_table_words(tab2_words, "im_window", "then_im_words")
+        im_planes = gather_planes(im_scale_window, im_second_plane, "im_first_plane")
+        wi = wi + load_wi_side(1, "then_wi_side1")
+        side0 = [quantise(raw_side0[0][:], "wr00")]
+        re_words = [gather_words(re_window, h, "re_words%d" % h) for h in range(HALVES)]
+        side0.append(quantise(raw_side0[1][:], "wr01"))
+        raw_side1 = keep.tile([P, PASSES, PACK, WIDE], F32, name="raw_side1", tag="then_raw_side1", align_bytes=64)
         for a in range(PASSES):
-            nc.sync.dma_start(both1[:, a], wr_rows[a, :, :, M : 2 * M])
-        raw1 = [both1[:, a] for a in range(PASSES)]
-        both23 = keep.tile([P, PASSES, PACK, 2 * M], F32, name="raw23", tag="shared_b", align_bytes=64)
-        for a in range(PASSES):
-            nc.sync.dma_start(both23[:, a], wr_rows[a, :, :, 2 * M : 4 * M])
-        raw23 = [both23[:, a] for a in range(PASSES)]
+            nc.sync.dma_start(raw_side1[:, a], wr_rows[a, :, :, WIDE : 2 * WIDE])
+        wr_pos = chunks_of(side0, 0)
+        wr_neg = chunks_of(side0, 1)
 
-        tiles = [(c, h) for c in range(CHUNKS) for h in range(HALVES)]
-        free = list(range(8))
-        zi = {}
-        zr = {}
+        free_banks = list(range(BANKS))
 
-        def take(kind, t):
-            b = free.pop(0)
-            return b, psum.tile([M, HALF], F32, name="%s%d%d" % (kind, t[0], t[1]), tag="bank%d" % b)
-
-        early = sorted(tiles[:-1], key=lambda t: t[1])
-        for t in early:
-            zi[t] = take("zi", t)
-            product(zi[t][1], wi[t[0]], re[t[1]], re_planes, t[1], True, False)
-        zr[tiles[0]] = take("zr", tiles[0])
-        product(zr[tiles[0]][1], wq[0][1], re[0], re_planes, 0, True, False)
-
-        im = [gather_words(im_win, h, "im%d" % h) for h in range(HALVES)]
-        wq.append(quantise(raw1, 0, "wr1"))
+        def take_bank(name):
+            b = free_banks.pop(0)
+            return b, psum.tile([M, HALF], F32, name=name, tag="bank%d" % b)
 
         def square(slot, name):
-            sq = ring.tile([M, HALF], F32, name=name)
-            nc.scalar.activation(sq[:], slot[1][:], ACT.Square)
-            free.append(slot[0])
-            return sq
+            squared = ring.tile([M, HALF], F32, name=name, bufs=STAGES)
+            nc.scalar.activation(squared[:], slot[1][:], ACT.Square)
+            free_banks.append(slot[0])
+            return squared
 
-        for i, t in enumerate(tiles[:-1]):
-            c, h = t
-            if i in (2, 4):
-                wq.append(quantise(raw23, i // 2 - 1, "wr%d" % (i // 2 + 1)))
-            if i == 0:
-                product(zi[t][1], wq[c][0], im[h], im_planes, h, False, True)
-                zi_sq = square(zi[t], "zi_sq")
-                product(zr[t][1], wi[c], im[h], im_planes, h, False, True)
-            elif i == 1:
-                zr[t] = take("zr", t)
-                product(zr[t][1], wq[c][1], re[h], re_planes, h, True, False)
-                product(zi[t][1], wq[c][0], im[h], im_planes, h, False, True)
-                zi_sq = square(zi[t], "zi_sq")
-                product(zr[t][1], wi[c], im[h], im_planes, h, False, True)
-            else:
-                zr[t] = take("zr", t)
-                product(zr[t][1], wi[c], im[h], im_planes, h, True, False)
-                if i == 2:
-                    last = tiles[-1]
-                    zi[last] = take("zi", last)
-                    product(zi[last][1], wi[last[0]], re[last[1]], re_planes, last[1], True, False)
-                product(zi[t][1], wq[c][0], im[h], im_planes, h, False, True)
-                zi_sq = square(zi[t], "zi_sq")
-                product(zr[t][1], wq[c][1], re[h], re_planes, h, False, True)
-            zr_sq = square(zr[t], "zr_sq")
-            power = ring.tile([M, HALF], F32, name="power", bufs=4)
-            nc.vector.tensor_tensor(power[:], zr_sq[:], zi_sq[:], ALU.add)
+        def finish(zr_slot, zi_squared, c, h):
+            zr_squared = square(zr_slot, "zr_squared")
+            power = ring.tile([M, HALF], F32, name="power", bufs=STAGES)
+            nc.vector.tensor_tensor(power[:], zr_squared[:], zi_squared[:], ALU.add)
             nc.sync.dma_start(out[c * M : (c + 1) * M, h * HALF : (h + 1) * HALF], power[:])
 
-        c, h = tiles[-1]
-        product(zi[tiles[-1]][1], wq[c][0], im[h], im_planes, h, False, True)
-        zi_sq = square(zi[tiles[-1]], "zi_sq")
+        early = [(c, h) for h in range(HALVES) for c in range(SIDE_CHUNKS)]
+        late = [(c, h) for c in range(SIDE_CHUNKS, 2 * SIDE_CHUNKS) for h in range(HALVES)]
+        zi = {}
+        zr = {}
+        for c, h in early:
+            zi[c, h] = take_bank("zi%d%d" % (c, h))
+            product(zi[c, h][1], wi[c], re_words[h], re_planes, h, True, False)
+        for c, h in early:
+            zr[c, h] = take_bank("zr%d%d" % (c, h))
+            product(zr[c, h][1], wr_neg[c], re_words[h], re_planes, h, True, False)
+
+        im_words = [gather_words(im_window, h, "im_words%d" % h) for h in range(HALVES)]
+        side1 = [quantise(raw_side1[:, a], "wr1%d" % a) for a in range(PASSES)]
+        wr_pos = wr_pos + chunks_of(side1, 0)
+        wr_neg = wr_neg + chunks_of(side1, 1)
+
+        for c, h in early:
+            product(zi[c, h][1], wr_pos[c], im_words[h], im_planes, h, False, True)
+            zi_squared = square(zi[c, h], "zi_squared")
+            product(zr[c, h][1], wi[c], im_words[h], im_planes, h, False, True)
+            finish(zr[c, h], zi_squared, c, h)
+
+        def whole_zi(c, h):
+            slot = take_bank("zi%d%d" % (c, h))
+            product(slot[1], wi[c], re_words[h], re_planes, h, True, False)
+            product(slot[1], wr_pos[c], im_words[h], im_planes, h, False, True)
+            return square(slot, "zi_squared")
+
+        for c, h in late[:-1]:
+            zi_squared = whole_zi(c, h)
+            zr_slot = take_bank("zr%d%d" % (c, h))
+            product(zr_slot[1], wi[c], im_words[h], im_planes, h, True, False)
+            product(zr_slot[1], wr_neg[c], re_words[h], re_planes, h, False, True)
+            finish(zr_slot, zi_squared, c, h)
+
+        c, h = late[-1]
+        zi_squared = whole_zi(c, h)
         for j0 in range(0, HALF, M):
-            b, bank = take("zr_end", (c, j0 // M))
-            product(bank, wi[c], im[h], im_planes, h, True, False, j0, j0 + M)
-            product(bank, wq[c][1], re[h], re_planes, h, False, True, j0, j0 + M)
-            zr_end = ring.tile([M, M], F32, name="zr_end", bufs=4)
-            nc.scalar.activation(zr_end[:], bank[:, 0:M], ACT.Square)
-            power_end = ring.tile([M, M], F32, name="power_end", bufs=4)
-            nc.vector.tensor_tensor(power_end[:], zr_end[:], zi_sq[:, j0 : j0 + M], ALU.add)
-            nc.sync.dma_start(out[c * M : (c + 1) * M, h * HALF + j0 : h * HALF + j0 + M], power_end[:])
+            bank = take_bank("zr_piece%d" % (j0 // M))[1]
+            product(bank, wi[c], im_words[h], im_planes, h, True, False, j0, j0 + M)
+            product(bank, wr_neg[c], re_words[h], re_planes, h, False, True, j0, j0 + M)
+            piece_squared = ring.tile([M, M], F32, name="piece_squared", bufs=STAGES)
+            nc.scalar.activation(piece_squared[:], bank[:, 0:M], ACT.Square)
+            piece_power = ring.tile([M, M], F32, name="piece_power", bufs=STAGES)
+            nc.vector.tensor_tensor(piece_power[:], piece_squared[:], zi_squared[:, j0 : j0 + M], ALU.add)
+            nc.sync.dma_start(out[c * M : (c + 1) * M, h * HALF + j0 : h * HALF + j0 + M], piece_power[:])

from contextlib import ExitStack

import concourse.mybir as mybir

K, N, T, J = 1024, 512, 4096, 1024
FLOPS = 4 * 2 * K * N * J

F32 = mybir.dt.float32
BF16 = mybir.dt.bfloat16
I32 = mybir.dt.int32
U32 = mybir.dt.uint32
U16 = mybir.dt.uint16
U8 = mybir.dt.uint8
FP8X4 = mybir.dt.float8_e4m3fn_x4
FP4X4 = mybir.dt.float4_e2m1fn_x4
ALU = mybir.AluOpType
ACT = mybir.ActivationFunctionType

P = 128
PACK = 4
PASSES = K // (P * PACK)
LIVE_ROWS = 4
SECOND_PASS_ROW = 16
LIST_ROWS = 16
M = 128
HALF = 512
HALVES = J // HALF
BANKS = 8
SIDE_CHUNKS = BANKS // (2 * HALVES)
WIDE = SIDE_CHUNKS * M
LINE = 4
STAGES = 4


def tile_list_cpxtab_pow_kernel(
    tc, tab_words, tab_scales, tab2_words, tab2_scales, wr, wi_words, wi_scales, offs, out
):
    nc = tc.nc
    with ExitStack() as ctx:
        keep = ctx.enter_context(tc.tile_pool(name="keep", bufs=1))
        ring = ctx.enter_context(tc.tile_pool(name="ring", bufs=2))
        psum = ctx.enter_context(tc.psum_pool(name="psum", bufs=1))

        offsets = keep.tile([P, J // LIST_ROWS], U16, name="offsets")
        nc.sync.dma_start(offsets[:], offs)

        def zeroed(columns, name, tag):
            cleared = keep.tile([P, columns], U8, name=name, tag=tag, align_bytes=64)
            nc.vector.memset(cleared[:].bitcast(I32), 0)
            return cleared

        def load_table_words(words, name, tag):
            window = keep.tile([P, T], I32, name=name, tag=tag, align_bytes=64)
            nc.sync.dma_start(window[:], words[0].rearrange("p t b -> p (t b)").bitcast(I32))
            return window

        def load_table_scales(window, scales):
            rows = scales.rearrange("a (q r) t -> r q a t", r=LIVE_ROWS)
            for r in range(LIVE_ROWS):
                nc.sync.dma_start(window[r:P:SECOND_PASS_ROW, :].bitcast(I32), rows[r].bitcast(I32))

        def gather_planes(window, second, name):
            first = keep.tile([P, J], U8, name=name, align_bytes=64)
            nc.vector.tensor_copy(first[:], window[:].indirect(offsets[:]))
            nc.sync.dma_start(
                second[0 : P - SECOND_PASS_ROW, :].bitcast(I32), first[SECOND_PASS_ROW:P, :].bitcast(I32)
            )
            return [first, second]

        def gather_words(window, h, name):
            pairs = keep.tile([P, HALF], I32, name="pairs", align_bytes=64)
            entries = slice(h * HALF // LIST_ROWS, (h + 1) * HALF // LIST_ROWS)
            nc.vector.tensor_copy(pairs[:].bitcast(U32), window[:].bitcast(U32).indirect(offsets[:, entries]))
            by_pass = pairs[:].bitcast(U16).rearrange("p (j a) -> p a j", a=PASSES)
            parted = []
            for a in range(PASSES):
                words = keep.tile([P, HALF], U16, name="%s_%d" % (name, a), align_bytes=64)
                nc.vector.tensor_copy(words[:], by_pass[:, a, :])
                parted.append(words)
            return parted

        wr_rows = wr.rearrange("(a p t) n -> a p t n", a=PASSES, t=PACK)
        wi_by_partition = wi_words.rearrange("a p n t -> p a (n t)").bitcast(I32)

        def load_wi_side(side, tag):
            codes = keep.tile([P, PASSES, WIDE], I32, name="wi_codes%d" % side, tag=tag, align_bytes=64)
            nc.sync.dma_start(codes[:], wi_by_partition[:, :, side * WIDE : (side + 1) * WIDE])
            chunks = []
            for u in range(SIDE_CHUNKS):
                n0 = side * WIDE + u * M
                chunks.append(
                    [(codes[:, a, u * M : (u + 1) * M], wi_planes[:, a * N + n0 : a * N + n0 + M]) for a in range(PASSES)]
                )
            return chunks

        def quantise(raw, name):
            pos = ring.tile([P, WIDE, PACK], BF16, name="pos", align_bytes=64)
            neg = ring.tile([P, WIDE, PACK], BF16, name="neg", align_bytes=64)
            nc.scalar.copy(
                pos[:].rearrange("p (c i) t -> p c t i", i=LINE), raw.rearrange("p t (c i) -> p c t i", i=LINE)
            )
            flat_pos = pos[:].rearrange("p n t -> p (n t)")
            flat_neg = neg[:].rearrange("p n t -> p (n t)")
            nc.vector.tensor_scalar(flat_neg, flat_pos, -1.0, None, ALU.mult)
            signs = []
            for flat, sign in ((flat_pos, "pos"), (flat_neg, "neg")):
                codes = keep.tile([P, WIDE], U32, name=name + sign + "_codes", align_bytes=64)
                plane = keep.tile([P, WIDE], U8, name=name + sign + "_plane", align_bytes=64)
                nc.vector.quantize_mx(out=codes[:].bitcast(FP8X4), scales=plane[:], in_=flat)
                signs.append((codes, plane))
            return signs

        def chunks_of(quantised, sign):
            return [
                [[part[:, u * M : (u + 1) * M] for part in quantised[a][sign]] for a in range(PASSES)]
                for u in range(SIDE_CHUNKS)
            ]

        def product(bank, weight, words, planes, h, start, stop, j0=0, j1=HALF):
            for a in range(PASSES):
                nc.tensor.matmul_mx(
                    out=bank[:, 0 : j1 - j0],
                    lhsT=weight[a][0].bitcast(FP8X4),
                    lhsT_scale=weight[a][1],
                    rhs=words[a][:, j0:j1].bitcast(FP4X4),
                    rhs_scale=planes[a][:, h * HALF + j0 : h * HALF + j1],
                    start=start and a == 0,
                    stop=stop and a == PASSES - 1,
                )

        re_scale_window = zeroed(T, "re_scale_window", "then_im_words")
        im_scale_window = zeroed(T, "im_scale_window", "then_wi_side1")
        wi_planes = zeroed(PASSES * N, "wi_planes", "wi_planes")
        re_second_plane = zeroed(J, "re_second_plane", "re_second_plane")
        im_second_plane = zeroed(J, "im_second_plane", "im_second_plane")

        wi = load_wi_side(0, "wi_side0")
        raw_side0 = [keep.tile([P, PACK, WIDE], F32, name="raw_side0_%d" % a, align_bytes=64) for a in range(PASSES)]
        nc.sync.dma_start(raw_side0[0][:], wr_rows[0, :, :, 0:WIDE])
        load_table_scales(re_scale_window, tab_scales)
        load_table_scales(im_scale_window, tab2_scales)
        wi_scale_rows = wi_scales.rearrange("a (q r) n -> r q a n", r=LIVE_ROWS)
        for r in range(LIVE_ROWS):
            nc.sync.dma_start(
                wi_planes[r:P:32, :].bitcast(I32).rearrange("q (a n) -> q a n", a=PASSES),
                wi_scale_rows[r].bitcast(I32),
            )
        re_window = load_table_words(tab_words, "re_window", "then_raw_side1")
        nc.sync.dma_start(raw_side0[1][:], wr_rows[1, :, :, 0:WIDE])

        re_planes = gather_planes(re_scale_window, re_second_plane, "re_first_plane")
        im_window = load_table_words(tab2_words, "im_window", "then_im_words")
        im_planes = gather_planes(im_scale_window, im_second_plane, "im_first_plane")
        wi = wi + load_wi_side(1, "then_wi_side1")
        side0 = [quantise(raw_side0[0][:], "wr00")]
        re_words = [gather_words(re_window, h, "re_words%d" % h) for h in range(HALVES)]
        side0.append(quantise(raw_side0[1][:], "wr01"))
        raw_side1 = keep.tile([P, PASSES, PACK, WIDE], F32, name="raw_side1", tag="then_raw_side1", align_bytes=64)
        for a in range(PASSES):
            nc.sync.dma_start(raw_side1[:, a], wr_rows[a, :, :, WIDE : 2 * WIDE])
        wr_pos = chunks_of(side0, 0)
        wr_neg = chunks_of(side0, 1)

        free_banks = list(range(BANKS))

        def take_bank(name):
            b = free_banks.pop(0)
            return b, psum.tile([M, HALF], F32, name=name, tag="bank%d" % b)

        def square(slot, name):
            squared = ring.tile([M, HALF], F32, name=name, bufs=STAGES)
            nc.scalar.activation(squared[:], slot[1][:], ACT.Square)
            free_banks.append(slot[0])
            return squared

        def finish(zr_slot, zi_squared, c, h):
            zr_squared = square(zr_slot, "zr_squared")
            power = ring.tile([M, HALF], F32, name="power", bufs=STAGES)
            nc.vector.tensor_tensor(power[:], zr_squared[:], zi_squared[:], ALU.add)
            nc.sync.dma_start(out[c * M : (c + 1) * M, h * HALF : (h + 1) * HALF], power[:])

        early = [(c, h) for h in range(HALVES) for c in range(SIDE_CHUNKS)]
        late = [(c, h) for c in range(SIDE_CHUNKS, 2 * SIDE_CHUNKS) for h in range(HALVES)]
        zi = {}
        zr = {}
        for c, h in early:
            zi[c, h] = take_bank("zi%d%d" % (c, h))
            product(zi[c, h][1], wi[c], re_words[h], re_planes, h, True, False)
        for c, h in early:
            zr[c, h] = take_bank("zr%d%d" % (c, h))
            product(zr[c, h][1], wr_neg[c], re_words[h], re_planes, h, True, False)

        im_words = [gather_words(im_window, h, "im_words%d" % h) for h in range(HALVES)]
        side1 = [quantise(raw_side1[:, a], "wr1%d" % a) for a in range(PASSES)]
        wr_pos = wr_pos + chunks_of(side1, 0)
        wr_neg = wr_neg + chunks_of(side1, 1)

        for c, h in early:
            product(zi[c, h][1], wr_pos[c], im_words[h], im_planes, h, False, True)
            zi_squared = square(zi[c, h], "zi_squared")
            product(zr[c, h][1], wi[c], im_words[h], im_planes, h, False, True)
            finish(zr[c, h], zi_squared, c, h)

        def whole_zi(c, h):
            slot = take_bank("zi%d%d" % (c, h))
            product(slot[1], wi[c], re_words[h], re_planes, h, True, False)
            product(slot[1], wr_pos[c], im_words[h], im_planes, h, False, True)
            return square(slot, "zi_squared")

        for c, h in late[:-1]:
            zi_squared = whole_zi(c, h)
            zr_slot = take_bank("zr%d%d" % (c, h))
            product(zr_slot[1], wi[c], im_words[h], im_planes, h, True, False)
            product(zr_slot[1], wr_neg[c], re_words[h], re_planes, h, False, True)
            finish(zr_slot, zi_squared, c, h)

        c, h = late[-1]
        zi_squared = whole_zi(c, h)
        for j0 in range(0, HALF, M):
            bank = take_bank("zr_piece%d" % (j0 // M))[1]
            product(bank, wi[c], im_words[h], im_planes, h, True, False, j0, j0 + M)
            product(bank, wr_neg[c], re_words[h], re_planes, h, False, True, j0, j0 + M)
            piece_squared = ring.tile([M, M], F32, name="piece_squared", bufs=STAGES)
            nc.scalar.activation(piece_squared[:], bank[:, 0:M], ACT.Square)
            piece_power = ring.tile([M, M], F32, name="piece_power", bufs=STAGES)
            nc.vector.tensor_tensor(piece_power[:], piece_squared[:], zi_squared[:, j0 : j0 + M], ALU.add)
            nc.sync.dma_start(out[c * M : (c + 1) * M, h * HALF + j0 : h * HALF + j0 + M], piece_power[:])
